import numpy as np
import ml_dtypes


def mxq(x, axis, fmt="e4m3"):
    dtype, down = {"e4m3": (ml_dtypes.float8_e4m3fn, 7), "e5m2": (ml_dtypes.float8_e5m2, 14)}[fmt]
    v = np.moveaxis(np.asarray(x, np.float32).astype(ml_dtypes.bfloat16).astype(np.float64), axis, -1)
    blocks = v.reshape(v.shape[:-1] + (-1, 32))
    amax = np.abs(blocks).max(-1, keepdims=True)
    byte = np.maximum(np.where(amax > 0, np.frexp(amax)[1] - 1 + 127, 0) - down, 1)
    scale = np.exp2(byte - 127.0)
    codes = (blocks / scale).astype(np.float32).astype(dtype).astype(np.float64)
    return np.moveaxis((codes * scale).reshape(v.shape), -1, axis)


WIDE = False


def mx_kscale(k):
    if not WIDE:
        return np.ones(k)
    levels = np.array([10, -10, 5, -5, 0])
    if k % 512:
        return np.exp2(np.random.permutation(np.resize(levels, k // 32))).repeat(32)
    a = np.empty((k // 512, 16))
    for p in range(k // 512):
        a[p, :8] = np.random.permutation(np.resize(levels, 8))
        for g in range(8):
            far = levels[np.abs(levels - a[p, g]) >= 10]
            a[p, g + 8] = far[np.random.randint(len(far))]
    return np.exp2(a.ravel()).repeat(32)


def f64(x):
    return np.asarray(x).astype(np.float64)


def striped(idx):
    return np.tile(idx.reshape(-1, 16).T, (8, 1)).astype(np.uint16)


def unstriped(offs):
    return offs[:16].T.reshape(-1).astype(np.int64)


E2M1 = np.array([0.0, 0.5, 1.0, 1.5, 2.0, 3.0, 4.0, 6.0, -0.0, -0.5, -1.0, -1.5, -2.0, -3.0, -4.0, -6.0])


def pack_weight(w, fmt):
    k, n = w.shape
    w = f64(np.asarray(w, np.float32).astype(ml_dtypes.bfloat16)).reshape(k // 32, 32, n)
    amax = np.abs(w).max(1)
    if fmt == "e4m3":
        byte = np.frexp(amax)[1] - 1 + 127 - 7
    else:
        mant, ex = np.frexp(amax / 6.0)
        byte = np.where(mant > 0.5, ex, ex - 1) + 127
    byte = np.clip(np.where(amax > 0, byte, 1), 1, 254)
    scaled = (w * np.exp2(127.0 - byte)[:, None, :]).reshape(k, n).astype(np.float32)
    by_word = np.ascontiguousarray(scaled.reshape(k // 512, 128, 4, n).transpose(0, 1, 3, 2))
    if fmt == "e4m3":
        words = by_word.astype(ml_dtypes.float8_e4m3fn).view(np.uint8)
    else:
        c = by_word.astype(ml_dtypes.float4_e2m1fn).view(np.uint8) & 0xF
        words = (c[..., 0::2] | (c[..., 1::2] << 4)).reshape(k // 512, 128, 2 * n)
    return np.ascontiguousarray(words), np.ascontiguousarray(byte.astype(np.uint8).reshape(k // 512, 16, n))


def unpack_weight(words, scales, fmt):
    g, _, n = scales.shape
    words = np.ascontiguousarray(words).reshape(g, 128, n, -1)
    if fmt == "e4m3":
        vals = words.view(ml_dtypes.float8_e4m3fn).astype(np.float64)
    else:
        nib = np.empty((g, 128, n, 4), np.uint8)
        nib[..., 0::2] = words & 0xF
        nib[..., 1::2] = words >> 4
        vals = E2M1[nib]
    vals = vals * np.repeat(np.exp2(scales.astype(np.float64) - 127.0), 8, axis=1)[..., None]
    return vals.transpose(0, 1, 3, 2).reshape(g * 512, n)


def gelu(v):
    return 0.5 * v * (1.0 + np.tanh(np.sqrt(2.0 / np.pi) * (v + 0.044715 * v**3)))


K, T, S, H, T2, P, N = 1536, 2048, 512, 1024, 1024, 512, 512

def setup_inputs():
    n = np.random.standard_normal
    s = mx_kscale(K)[:, None]
    u = mx_kscale(H)[:, None]
    d = {}
    d["tab_words"], d["tab_scales"] = pack_weight(n((K, T)) * s, "e4m3")
    d["w1"] = (2.0 * n((K, H)) / K**0.5 / s).astype(np.float32)
    d["w2_words"], d["w2_scales"] = pack_weight(2.0 * n((K, H)) / K**0.5 / s, "e2m1")
    d["gain"] = (2.3 * np.exp(0.3 * n(H)) * u[:, 0]).astype(np.float32)
    d["wgs"] = np.exp(0.3 * n((128, S))).astype(np.float32)
    d["page0"] = (n((H, T2)) * u).astype(np.float32)
    d["want"] = (0.8 * n((H, P)) * u).astype(np.float32)
    d["w3"] = (n((H, N)) / H**0.5 / u).astype(np.float32)
    d["w4_words"], d["w4_scales"] = pack_weight(1.5 * n((H, N)) / H**0.5 / u, "e4m3")
    d["wgo"] = np.exp(0.3 * n((128, P))).astype(np.float32)
    d["page1"] = n((N, T2)).astype(np.float32)
    d["offs"] = striped(np.random.permutation(T)[:S])
    d["offs2"] = striped(np.random.permutation(T2)[:S])
    d["offs3"] = striped(np.random.permutation(T2)[:P])
    d["offs4"] = striped(np.random.permutation(T2)[:P])
    return d

def reference(tab_words, tab_scales, w1, w2_words, w2_scales, gain, wgs, page0, want, w3, w4_words, w4_scales, wgo, page1, offs, offs2, offs3, offs4):
    v = unpack_weight(tab_words, tab_scales, "e4m3")[:, unstriped(offs)]
    raised = mxq(f64(w1), 0, "e4m3").T @ v
    flat = unpack_weight(w2_words, w2_scales, "e2m1").T @ v
    h = (1.0 / (1.0 + np.exp(-raised)) - 1.0 / (1.0 + np.exp(-flat))) * f64(gain)[:, None]
    page = f64(page0).copy()
    page[:, unstriped(offs2)] = np.tile(f64(wgs), (H // 128, 1)) * h
    x = page[:, unstriped(offs3)] - f64(want)
    fix = mxq(f64(w3), 0, "e4m3").T @ mxq(x, 0, "e4m3")
    sway = unpack_weight(w4_words, w4_scales, "e4m3").T @ mxq(h, 0, "e4m3")
    y = fix * np.tanh(sway)
    out = f64(page1).copy()
    out[:, unstriped(offs4)] = np.tile(f64(wgo), (N // 128, 1)) * y
    return out

@@ -1,0 +1,283 @@
+from contextlib import ExitStack
+
+import concourse.mybir as mybir
+from concourse.masks import make_identity
+
+K, T, S, H, T2, N = 1536, 2048, 512, 1024, 1024, 512
+FLOPS = 2 * (2 * K * H * S + 2 * H * N * S)
+
+F32 = mybir.dt.float32
+BF16 = mybir.dt.bfloat16
+I32 = mybir.dt.int32
+U32 = mybir.dt.uint32
+U16 = mybir.dt.uint16
+U8 = mybir.dt.uint8
+FP8X4 = mybir.dt.float8_e4m3fn_x4
+FP4X4 = mybir.dt.float4_e2m1fn_x4
+ALU = mybir.AluOpType
+ACT = mybir.ActivationFunctionType
+
+P = 128
+PACK = 4
+PASS = P * PACK
+K_PASSES = K // PASS
+R_PASSES = H // PASS
+J_TILES = S // P
+N_TILES = N // P
+HALF = S // 2
+
+
+def tile_list_braille_proof_correction_kernel(
+    tc, tab_words, tab_scales, w1, w2_words, w2_scales, gain, wgs, page0, want, w3, w4_words, w4_scales,
+    wgo, page1, offs, offs2, offs3, offs4, out,
+):
+    nc = tc.nc
+    with ExitStack() as ctx:
+        keep = ctx.enter_context(tc.tile_pool(name="keep", bufs=1))
+        ring = ctx.enter_context(tc.tile_pool(name="ring", bufs=1))
+        bank_a = ctx.enter_context(tc.psum_pool(name="bank_a", bufs=4))
+        bank_b = ctx.enter_context(tc.psum_pool(name="bank_b", bufs=4))
+
+        def load_list(name, src):
+            tile = keep.tile([P, S // 16], U16, name=name)
+            nc.sync.dma_start(tile[:], src)
+            return tile
+
+        def load_scales(name, src, queue):
+            passes, width = src.shape[0], src.shape[2]
+            tile = keep.tile([P, passes * width], U8, name=name, align_bytes=64)
+            nc.vector.memset(tile[:].bitcast(I32), 0)
+            for q in range(4):
+                queue.dma_start(
+                    out=tile[32 * q : 32 * q + 4, :].bitcast(I32).rearrange("r (a c) -> r a c", a=passes),
+                    in_=src[:, 4 * q : 4 * q + 4, :].rearrange("a r c -> r a c").bitcast(I32),
+                )
+            return tile
+
+        def load_rows(src, tag="raw", bufs=3):
+            tile = ring.tile([P, PACK, src.shape[1]], F32, name=tag, tag=tag, bufs=bufs, align_bytes=64)
+            nc.sync.dma_start(out=tile[:], in_=src.rearrange("(p i) c -> p i c", i=PACK))
+            return tile
+
+        def interleave(engine_copy, raw, tag="grouped", bufs=3):
+            width = raw.shape[2]
+            grouped = ring.tile([P, width, PACK], BF16, name=tag, tag=tag, bufs=bufs, align_bytes=64)
+            engine_copy(
+                out=grouped[:].rearrange("p (c u) i -> p c i u", u=4),
+                in_=raw[:].rearrange("p i (c u) -> p c i u", u=4),
+            )
+            return grouped
+
+        def quantize(grouped, tag, bufs):
+            width = grouped.shape[1]
+            codes = ring.tile([P, width], U32, name=tag + "_codes", tag=tag + "_codes", bufs=bufs, align_bytes=64)
+            scales = ring.tile([P, width], U8, name=tag + "_scales", tag=tag + "_scales", bufs=bufs, align_bytes=64)
+            nc.vector.quantize_mx(
+                out=codes[:].bitcast(FP8X4), scales=scales[:], in_=grouped[:].rearrange("p c i -> p (c i)")
+            )
+            return codes, scales
+
+        def load_table(a):
+            tile = keep.tile([P, T], U32, name="tab%d" % a, align_bytes=64)
+            nc.sync.dma_start(out=tile[:].bitcast(I32), in_=tab_words[a].rearrange("p t i -> p (t i)").bitcast(I32))
+            return tile
+
+        def gather_table(a, words):
+            v_scale = keep.tile([P, S], U8, name="v_scale%d" % a, align_bytes=64)
+            nc.vector.tensor_copy(v_scale[:], tab_s[:, a * T : (a + 1) * T].indirect(idx[:]))
+            v_codes = keep.tile([P, S], U32, name="v_codes%d" % a, align_bytes=64)
+            nc.vector.tensor_copy(v_codes[:], words[:].indirect(idx[:]))
+            return v_codes, v_scale
+
+        def load_w1(a, b):
+            return load_rows(w1[a * PASS : (a + 1) * PASS, b * PASS : (b + 1) * PASS])
+
+        def load_w2(b):
+            tile = keep.tile([P, K_PASSES, 2 * PASS], U8, name="w2_%d" % b, align_bytes=64)
+            nc.sync.dma_start(
+                out=tile[:].bitcast(I32),
+                in_=w2_words[:, :, 2 * PASS * b : 2 * PASS * (b + 1)].rearrange("a p c -> p a c").bitcast(I32),
+            )
+            return tile
+
+        def load_page0(b, t):
+            tile = keep.tile([P, T2], F32, name="page0_%d_%d" % (b, t))
+            nc.sync.dma_start(
+                out=tile[:], in_=page0[b * PASS : (b + 1) * PASS, :].rearrange("(p t) c -> t p c", t=PACK)[t]
+            )
+            return tile
+
+        def first_stage_pass(banks, a, w_codes, w_scale):
+            v_codes, v_scale = v[a]
+            for jt in range(J_TILES):
+                cols = slice(jt * P, (jt + 1) * P)
+                nc.tensor.matmul_mx(
+                    out=banks[jt][:], lhsT=v_codes[:, cols].bitcast(FP8X4), lhsT_scale=v_scale[:, cols],
+                    rhs=w_codes, rhs_scale=w_scale, start=(a == 0), stop=(a == K_PASSES - 1),
+                )
+
+        def half_tanh(banks, scale):
+            tiles = []
+            for bank in banks:
+                tile = ring.tile([P, PACK, P], F32, name="th", tag="th", bufs=8)
+                nc.scalar.activation(
+                    out=tile[:], in_=bank[:].rearrange("j (m t) -> j t m", t=PACK), func=ACT.Tanh, scale=scale
+                )
+                tiles.append(tile)
+            return tiles
+
+        def flat_stage(b, w2_tile):
+            banks = [bank_a.tile([P, PASS], F32, name="a", tag="a") for jt in range(J_TILES)]
+            for a in range(K_PASSES):
+                first_stage_pass(
+                    banks, a, w2_tile[:, a, :].bitcast(FP4X4), w2_s[:, a * H + b * PASS : a * H + (b + 1) * PASS]
+                )
+            return half_tanh(banks, -0.5)
+
+        def raised_pass(banks, a, grouped):
+            codes, scales = quantize(grouped, "w1q", 3)
+            first_stage_pass(banks, a, codes[:].bitcast(FP8X4), scales[:])
+
+        def cell_states(b, th_raised, th_flat):
+            h = ring.tile([P, PACK, S], F32, name="h", tag="h", bufs=2)
+            for t in range(PACK):
+                bank = bank_a.tile([P, S], F32, name="a", tag="a")
+                for jt in range(J_TILES):
+                    cols = slice(jt * P, (jt + 1) * P)
+                    nc.tensor.matmul(
+                        bank[:, cols], th_flat[jt][:, t, :], ident[:], start=True, stop=False, is_transpose=True
+                    )
+                    nc.tensor.matmul(
+                        bank[:, cols], th_raised[jt][:, t, :], ident[:], start=False, stop=True, is_transpose=True
+                    )
+                nc.scalar.activation(out=h[:, t, :], in_=bank[:], func=ACT.Copy, scale=half_gain[:, b, t : t + 1])
+            return h
+
+        def scatter(page, offsets, values, weights):
+            nc.vector.tensor_tensor(page[:].indirect(offsets[:]), values, weights, ALU.mult)
+
+        def recall(x, pages, wanted, j0, width):
+            for t in range(PACK):
+                nc.vector.tensor_tensor(
+                    x[:, t, :], pages[t][:].indirect(idx3[:, j0 // 16 : (j0 + width) // 16]),
+                    wanted[:, t, j0 : j0 + width], ALU.subtract,
+                )
+
+        idx = load_list("idx", offs)
+        tab0 = load_table(0)
+        tab_s = load_scales("tab_s", tab_scales, nc.sync)
+        ident = keep.tile([P, P], F32, name="ident")
+        make_identity(nc, ident[:])
+        w2_s = load_scales("w2_s", w2_scales, nc.gpsimd)
+        w4_s = load_scales("w4_s", w4_scales, nc.gpsimd)
+        tab1 = load_table(1)
+        w1_00 = load_w1(0, 0)
+        tab2 = load_table(2)
+        w2_0 = load_w2(0)
+        w1_10 = load_w1(1, 0)
+        w1_20 = load_w1(2, 0)
+        gain_t = keep.tile([P, R_PASSES, PACK], F32, name="gain_t")
+        nc.sync.dma_start(out=gain_t[:], in_=gain.rearrange("(b p t) -> p b t", b=R_PASSES, t=PACK))
+        half_gain = keep.tile([P, R_PASSES, PACK], F32, name="half_gain")
+        nc.scalar.activation(out=half_gain[:], in_=gain_t[:], func=ACT.Copy, scale=0.5)
+        idx2 = load_list("idx2", offs2)
+        wgs_t = keep.tile([P, PACK, S], F32, name="wgs_t")
+        for q in (0, 2, 1, 3):
+            nc.sync.dma_start(out=wgs_t[32 * q : 32 * q + 32], in_=wgs.rearrange("(m t) j -> m t j", t=PACK))
+        pages = [[load_page0(0, 0)], []]
+        w1_01 = load_w1(0, 1)
+        pages[0].append(load_page0(0, 1))
+        w2_1 = load_w2(1)
+        w1_11 = load_w1(1, 1)
+        pages[0].append(load_page0(0, 2))
+        w1_21 = load_w1(2, 1)
+        pages[0].append(load_page0(0, 3))
+
+        v = [gather_table(a, words) for a, words in enumerate((tab0, tab1, tab2))]
+        g_00 = interleave(nc.scalar.copy, w1_00)
+        th_flat = flat_stage(0, w2_0)
+        raised = [bank_b.tile([P, PASS], F32, name="b", tag="b") for jt in range(J_TILES)]
+        raised_pass(raised, 0, g_00)
+        raised_pass(raised, 1, interleave(nc.vector.tensor_copy, w1_10))
+        raised_pass(raised, 2, interleave(nc.vector.tensor_copy, w1_20))
+        h0 = cell_states(0, half_tanh(raised, 0.5), th_flat)
+
+        idx3 = load_list("idx3", offs3)
+        idx4 = load_list("idx4", offs4)
+        want0 = load_rows(want[0:PASS, :])
+        pages[1].append(load_page0(1, 0))
+        w4_t = keep.tile([P, R_PASSES, N], U32, name="w4_t", align_bytes=64)
+        nc.sync.dma_start(out=w4_t[:].bitcast(I32), in_=w4_words.rearrange("a p c i -> p a (c i)").bitcast(I32))
+        w3_0 = load_rows(w3[0:PASS, :])
+        pages[1].append(load_page0(1, 1))
+        pages[1].append(load_page0(1, 2))
+        w3_1 = load_rows(w3[PASS:H, :])
+        pages[1].append(load_page0(1, 3))
+        want1 = load_rows(want[PASS:H, :], tag="want1_then_factor", bufs=1)
+        wgo_t = keep.tile([P, S], F32, name="wgo_t")
+        nc.sync.dma_start(out=wgo_t[:], in_=wgo)
+        out_pages = []
+        for n in range(N_TILES):
+            tile = keep.tile([P, T2], F32, name="page1_%d" % n)
+            nc.sync.dma_start(out=tile[:], in_=page1[n * P : (n + 1) * P, :])
+            out_pages.append(tile)
+
+        raised = [bank_b.tile([P, PASS], F32, name="b", tag="b") for jt in range(J_TILES)]
+        raised_pass(raised, 0, interleave(nc.vector.tensor_copy, w1_01))
+        for t in range(PACK):
+            scatter(pages[0][t], idx2, h0[:, t, :], wgs_t[:, t, :])
+        raised_pass(raised, 1, interleave(nc.scalar.copy, w1_11))
+        raised_pass(raised, 2, interleave(nc.scalar.copy, w1_21, tag="w1_last_then_x0", bufs=1))
+        th_flat = flat_stage(1, w2_1)
+        h1 = cell_states(1, half_tanh(raised, 0.5), th_flat)
+        hq0 = quantize(interleave(nc.scalar.copy, h0), "hq", 2)
+
+        x0 = ring.tile([P, PACK, S], F32, name="x0", tag="w1_last_then_x0", bufs=1, align_bytes=64)
+        recall(x0, pages[0], want0, 0, S)
+        for t in range(PACK):
+            scatter(pages[1][t], idx2, h1[:, t, :], wgs_t[:, t, :])
+        hq1 = quantize(interleave(nc.scalar.copy, h1, tag="h1_then_x0", bufs=1), "hq", 2)
+        w3q = [quantize(interleave(nc.scalar.copy, raw), "w3q", 2) for raw in (w3_0, w3_1)]
+        xq0 = quantize(interleave(nc.scalar.copy, x0, tag="h1_then_x0", bufs=1), "xq0", 1)
+
+        sway = []
+        for n in range(N_TILES):
+            cols = slice(n * P, (n + 1) * P)
+            bank = bank_b.tile([P, S], F32, name="b", tag="b")
+            for b, (codes, scales) in enumerate((hq0, hq1)):
+                nc.tensor.matmul_mx(
+                    out=bank[:], lhsT=w4_t[:, b, cols].bitcast(FP8X4),
+                    lhsT_scale=w4_s[:, b * N + n * P : b * N + (n + 1) * P],
+                    rhs=codes[:].bitcast(FP8X4), rhs_scale=scales[:], start=(b == 0), stop=(b == R_PASSES - 1),
+                )
+            tile = ring.tile([P, S], F32, name="th", tag="th", bufs=8)
+            nc.scalar.activation(out=tile[:], in_=bank[:], func=ACT.Tanh)
+            sway.append(tile)
+
+        def fix_pass(bank, n, b, xq, j0, width, start, stop):
+            cols = slice(n * P, (n + 1) * P)
+            nc.tensor.matmul_mx(
+                out=bank[:, j0 : j0 + width], lhsT=w3q[b][0][:, cols].bitcast(FP8X4), lhsT_scale=w3q[b][1][:, cols],
+                rhs=xq[0][:].bitcast(FP8X4), rhs_scale=xq[1][:], start=start, stop=stop,
+            )
+
+        fix = [bank_a.tile([P, S], F32, name="a", tag="a") for n in range(N_TILES)]
+        for n in range(N_TILES):
+            fix_pass(fix[n], n, 0, xq0, 0, S, True, False)
+
+        xq1 = []
+        for half in range(2):
+            x1 = ring.tile([P, PACK, HALF], F32, name="h", tag="h", bufs=2)
+            recall(x1, pages[1], want1, half * HALF, HALF)
+            xq1.append(quantize(interleave(nc.scalar.copy, x1, tag="x1g", bufs=2), "xq1", 2))
+        factor = ring.tile([P, N_TILES, S], F32, name="factor", tag="want1_then_factor", bufs=1, align_bytes=64)
+        for n in range(N_TILES):
+            nc.vector.tensor_tensor(factor[:, n, :], sway[n][:], wgo_t[:], ALU.mult)
+        for half in range(2):
+            for n in range(N_TILES):
+                fix_pass(fix[n], n, 1, xq1[half], half * HALF, HALF, False, half == 1)
+        for n in range(N_TILES):
+            fix_sb = ring.tile([P, S], F32, name="th", tag="th", bufs=8)
+            nc.scalar.copy(out=fix_sb[:], in_=fix[n][:])
+            scatter(out_pages[n], idx4, fix_sb[:], factor[:, n, :])
+            nc.sync.dma_start(out=out[n * P : (n + 1) * P, :], in_=out_pages[n][:])

@@ -83,10 +83,10 @@ def tile_list_braille_proof_correction_kernel(
             return tile
 
         def gather_table(a, words):
-            v_scale = keep.tile([P, S], U8, name="v_scale%d" % a, align_bytes=64)
-            nc.vector.tensor_copy(v_scale[:], tab_s[:, a * T : (a + 1) * T].indirect(idx[:]))
             v_codes = keep.tile([P, S], U32, name="v_codes%d" % a, align_bytes=64)
             nc.vector.tensor_copy(v_codes[:], words[:].indirect(idx[:]))
+            v_scale = keep.tile([P, S], U8, name="v_scale%d" % a, align_bytes=64)
+            nc.vector.tensor_copy(v_scale[:], tab_s[:, a * T : (a + 1) * T].indirect(idx[:]))
             return v_codes, v_scale
 
         def load_w1(a, b):
@@ -107,21 +107,23 @@ def tile_list_braille_proof_correction_kernel(
             )
             return tile
 
-        def first_stage_pass(banks, a, w_codes, w_scale):
+        def first_stage_pass(banks, a, w_codes, w_scale, r0=0, width=PASS, stop=None):
             v_codes, v_scale = v[a]
             for jt in range(J_TILES):
                 cols = slice(jt * P, (jt + 1) * P)
                 nc.tensor.matmul_mx(
-                    out=banks[jt][:], lhsT=v_codes[:, cols].bitcast(FP8X4), lhsT_scale=v_scale[:, cols],
-                    rhs=w_codes, rhs_scale=w_scale, start=(a == 0), stop=(a == K_PASSES - 1),
+                    out=banks[jt][:, r0 : r0 + width], lhsT=v_codes[:, cols].bitcast(FP8X4),
+                    lhsT_scale=v_scale[:, cols], rhs=w_codes, rhs_scale=w_scale, start=(a == 0),
+                    stop=(a == K_PASSES - 1 if stop is None else stop),
                 )
 
-        def half_tanh(banks, scale):
+        def half_tanh(banks, scale, t0=0, t1=PACK, tag="th", bufs=8):
             tiles = []
             for bank in banks:
-                tile = ring.tile([P, PACK, P], F32, name="th", tag="th", bufs=8)
+                tile = ring.tile([P, t1 - t0, P], F32, name=tag, tag=tag, bufs=bufs)
                 nc.scalar.activation(
-                    out=tile[:], in_=bank[:].rearrange("j (m t) -> j t m", t=PACK), func=ACT.Tanh, scale=scale
+                    out=tile[:], in_=bank[:].rearrange("j (m t) -> j t m", t=PACK)[:, t0:t1, :], func=ACT.Tanh,
+                    scale=scale,
                 )
                 tiles.append(tile)
             return tiles
@@ -130,7 +132,7 @@ def tile_list_braille_proof_correction_kernel(
             banks = [bank_a.tile([P, PASS], F32, name="a", tag="a") for jt in range(J_TILES)]
             for a in range(K_PASSES):
                 first_stage_pass(
-                    banks, a, w2_tile[:, a, :].bitcast(FP4X4), w2_s[:, a * H + b * PASS : a * H + (b + 1) * PASS]
+                    banks, a, w2_tile[:, a, :].bitcast(FP4X4), w2_s[b][:, a * PASS : (a + 1) * PASS]
                 )
             return half_tanh(banks, -0.5)
 
@@ -138,20 +140,26 @@ def tile_list_braille_proof_correction_kernel(
             codes, scales = quantize(grouped, "w1q", 3)
             first_stage_pass(banks, a, codes[:].bitcast(FP8X4), scales[:])
 
-        def cell_states(b, th_raised, th_flat):
-            h = ring.tile([P, PACK, S], F32, name="h", tag="h", bufs=2)
+        def open_difference(th_flat):
+            banks = [bank_a.tile([P, S], F32, name="a", tag="a") for t in range(PACK)]
             for t in range(PACK):
-                bank = bank_a.tile([P, S], F32, name="a", tag="a")
                 for jt in range(J_TILES):
-                    cols = slice(jt * P, (jt + 1) * P)
                     nc.tensor.matmul(
-                        bank[:, cols], th_flat[jt][:, t, :], ident[:], start=True, stop=False, is_transpose=True
+                        banks[t][:, jt * P : (jt + 1) * P], th_flat[jt][:, t, :], ident[:],
+                        start=(jt == 0), stop=False, is_transpose=True,
                     )
+            return banks
+
+        def close_difference(h, b, banks, th_raised, t0, t1):
+            for t in range(t0, t1):
+                for jt in range(J_TILES):
                     nc.tensor.matmul(
-                        bank[:, cols], th_raised[jt][:, t, :], ident[:], start=False, stop=True, is_transpose=True
+                        banks[t][:, jt * P : (jt + 1) * P], th_raised[jt][:, t - t0, :], ident[:],
+                        start=False, stop=(jt == J_TILES - 1), is_transpose=True,
                     )
-                nc.scalar.activation(out=h[:, t, :], in_=bank[:], func=ACT.Copy, scale=half_gain[:, b, t : t + 1])
-            return h
+                nc.scalar.activation(
+                    out=h[:, t, :], in_=banks[t][:], func=ACT.Copy, scale=half_gain[:, b, t : t + 1]
+                )
 
         def scatter(page, offsets, values, weights):
             nc.vector.tensor_tensor(page[:].indirect(offsets[:]), values, weights, ALU.mult)
@@ -168,44 +176,55 @@ def tile_list_braille_proof_correction_kernel(
         tab_s = load_scales("tab_s", tab_scales, nc.sync)
         ident = keep.tile([P, P], F32, name="ident")
         make_identity(nc, ident[:])
-        w2_s = load_scales("w2_s", w2_scales, nc.gpsimd)
-        w4_s = load_scales("w4_s", w4_scales, nc.gpsimd)
         tab1 = load_table(1)
-        w1_00 = load_w1(0, 0)
         tab2 = load_table(2)
         w2_0 = load_w2(0)
+        w2_s = [load_scales("w2_s0", w2_scales[:, :, 0:PASS], nc.sync)]
+        w1_00 = load_w1(0, 0)
         w1_10 = load_w1(1, 0)
-        w1_20 = load_w1(2, 0)
+        w1_20 = [
+            load_rows(w1[2 * PASS : K, c0 : c0 + HALF], tag="raw_half", bufs=2) for c0 in (0, HALF)
+        ]
         gain_t = keep.tile([P, R_PASSES, PACK], F32, name="gain_t")
         nc.sync.dma_start(out=gain_t[:], in_=gain.rearrange("(b p t) -> p b t", b=R_PASSES, t=PACK))
         half_gain = keep.tile([P, R_PASSES, PACK], F32, name="half_gain")
         nc.scalar.activation(out=half_gain[:], in_=gain_t[:], func=ACT.Copy, scale=0.5)
         idx2 = load_list("idx2", offs2)
-        wgs_t = keep.tile([P, PACK, S], F32, name="wgs_t")
+        wgs_first = keep.tile([P, 1, S], F32, name="wgs_first")
+        wgs_rest = keep.tile([P, PACK - 1, S], F32, name="wgs_rest")
+        wgs_rows = wgs.rearrange("(m t) j -> m t j", t=PACK)
         for q in (0, 2, 1, 3):
-            nc.sync.dma_start(out=wgs_t[32 * q : 32 * q + 32], in_=wgs.rearrange("(m t) j -> m t j", t=PACK))
+            nc.sync.dma_start(out=wgs_first[32 * q : 32 * q + 32], in_=wgs_rows[:, 0:1, :])
+        wgs_t = [wgs_first[:, 0, :]] + [wgs_rest[:, t, :] for t in range(PACK - 1)]
         pages = [[load_page0(0, 0)], []]
         w1_01 = load_w1(0, 1)
+        for q in (0, 2, 1, 3):
+            nc.sync.dma_start(out=wgs_rest[32 * q : 32 * q + 32], in_=wgs_rows[:, 1:PACK, :])
         pages[0].append(load_page0(0, 1))
         w2_1 = load_w2(1)
+        w2_s.append(load_scales("w2_s1", w2_scales[:, :, PASS:H], nc.sync))
         w1_11 = load_w1(1, 1)
         pages[0].append(load_page0(0, 2))
         w1_21 = load_w1(2, 1)
         pages[0].append(load_page0(0, 3))
 
         v = [gather_table(a, words) for a, words in enumerate((tab0, tab1, tab2))]
-        g_00 = interleave(nc.scalar.copy, w1_00)
-        th_flat = flat_stage(0, w2_0)
+        diff = open_difference(flat_stage(0, w2_0))
         raised = [bank_b.tile([P, PASS], F32, name="b", tag="b") for jt in range(J_TILES)]
-        raised_pass(raised, 0, g_00)
+        raised_pass(raised, 0, interleave(nc.vector.tensor_copy, w1_00))
         raised_pass(raised, 1, interleave(nc.vector.tensor_copy, w1_10))
-        raised_pass(raised, 2, interleave(nc.vector.tensor_copy, w1_20))
-        h0 = cell_states(0, half_tanh(raised, 0.5), th_flat)
+        for half in range(2):
+            codes, scales = quantize(interleave(nc.vector.tensor_copy, w1_20[half], tag="x1g", bufs=2), "xq1", 2)
+            first_stage_pass(raised, 2, codes[:].bitcast(FP8X4), scales[:], half * HALF, HALF, half == 1)
+        h0 = ring.tile([P, PACK, S], F32, name="h", tag="h", bufs=2)
+        close_difference(h0, 0, diff, half_tanh(raised, 0.5, 0, 1, "th_first", 4), 0, 1)
+        close_difference(h0, 0, diff, half_tanh(raised, 0.5, 1, PACK), 1, PACK)
 
         idx3 = load_list("idx3", offs3)
         idx4 = load_list("idx4", offs4)
         want0 = load_rows(want[0:PASS, :])
         pages[1].append(load_page0(1, 0))
+        w4_s = load_scales("w4_s", w4_scales, nc.sync)
         w4_t = keep.tile([P, R_PASSES, N], U32, name="w4_t", align_bytes=64)
         nc.sync.dma_start(out=w4_t[:].bitcast(I32), in_=w4_words.rearrange("a p c i -> p a (c i)").bitcast(I32))
         w3_0 = load_rows(w3[0:PASS, :])
@@ -223,19 +242,20 @@ def tile_list_braille_proof_correction_kernel(
             out_pages.append(tile)
 
         raised = [bank_b.tile([P, PASS], F32, name="b", tag="b") for jt in range(J_TILES)]
-        raised_pass(raised, 0, interleave(nc.vector.tensor_copy, w1_01))
+        raised_pass(raised, 0, interleave(nc.scalar.copy, w1_01))
         for t in range(PACK):
-            scatter(pages[0][t], idx2, h0[:, t, :], wgs_t[:, t, :])
+            scatter(pages[0][t], idx2, h0[:, t, :], wgs_t[t])
+        diff = open_difference(flat_stage(1, w2_1))
         raised_pass(raised, 1, interleave(nc.scalar.copy, w1_11))
         raised_pass(raised, 2, interleave(nc.scalar.copy, w1_21, tag="w1_last_then_x0", bufs=1))
-        th_flat = flat_stage(1, w2_1)
-        h1 = cell_states(1, half_tanh(raised, 0.5), th_flat)
+        h1 = ring.tile([P, PACK, S], F32, name="h", tag="h", bufs=2)
+        close_difference(h1, 1, diff, half_tanh(raised, 0.5), 0, PACK)
         hq0 = quantize(interleave(nc.scalar.copy, h0), "hq", 2)
 
         x0 = ring.tile([P, PACK, S], F32, name="x0", tag="w1_last_then_x0", bufs=1, align_bytes=64)
         recall(x0, pages[0], want0, 0, S)
         for t in range(PACK):
-            scatter(pages[1][t], idx2, h1[:, t, :], wgs_t[:, t, :])
+            scatter(pages[1][t], idx2, h1[:, t, :], wgs_t[t])
         hq1 = quantize(interleave(nc.scalar.copy, h1, tag="h1_then_x0", bufs=1), "hq", 2)
         w3q = [quantize(interleave(nc.scalar.copy, raw), "w3q", 2) for raw in (w3_0, w3_1)]
         xq0 = quantize(interleave(nc.scalar.copy, x0, tag="h1_then_x0", bufs=1), "xq0", 1)

@@ -43,14 +43,15 @@ def tile_list_braille_proof_correction_kernel(
             nc.sync.dma_start(tile[:], src)
             return tile
 
-        def load_scales(name, src, queue):
+        def load_scales(name, src):
             passes, width = src.shape[0], src.shape[2]
             tile = keep.tile([P, passes * width], U8, name=name, align_bytes=64)
             nc.vector.memset(tile[:].bitcast(I32), 0)
-            for q in range(4):
-                queue.dma_start(
-                    out=tile[32 * q : 32 * q + 4, :].bitcast(I32).rearrange("r (a c) -> r a c", a=passes),
-                    in_=src[:, 4 * q : 4 * q + 4, :].rearrange("a r c -> r a c").bitcast(I32),
+            rows = src.rearrange("a (q r) c -> r q a c", r=4)
+            for r in range(4):
+                nc.sync.dma_start(
+                    out=tile[r:P:32, :].bitcast(I32).rearrange("q (a c) -> q a c", a=passes),
+                    in_=rows[r].bitcast(I32),
                 )
             return tile
 
@@ -91,6 +92,12 @@ def tile_list_braille_proof_correction_kernel(
 
         def load_w1(a, b):
             return load_rows(w1[a * PASS : (a + 1) * PASS, b * PASS : (b + 1) * PASS])
+
+        def load_w1_halves(b):
+            return [
+                load_rows(w1[2 * PASS : K, c0 : c0 + HALF], tag="raw_half", bufs=2)
+                for c0 in (b * PASS, b * PASS + HALF)
+            ]
 
         def load_w2(b):
             tile = keep.tile([P, K_PASSES, 2 * PASS], U8, name="w2_%d" % b, align_bytes=64)
@@ -173,40 +180,47 @@ def tile_list_braille_proof_correction_kernel(
 
         idx = load_list("idx", offs)
         tab0 = load_table(0)
-        tab_s = load_scales("tab_s", tab_scales, nc.sync)
+        tab_s = load_scales("tab_s", tab_scales)
+        wgs_rows = ring.tile([P, S], F32, name="th", tag="th", bufs=8)
+        nc.sync.dma_start(out=wgs_rows[:], in_=wgs)
         ident = keep.tile([P, P], F32, name="ident")
         make_identity(nc, ident[:])
+        gain_t = keep.tile([P, R_PASSES, PACK], F32, name="gain_t")
+        nc.gpsimd.dma_start(out=gain_t[:], in_=gain.rearrange("(b p t) -> p b t", b=R_PASSES, t=PACK))
         tab1 = load_table(1)
         tab2 = load_table(2)
         w2_0 = load_w2(0)
-        w2_s = [load_scales("w2_s0", w2_scales[:, :, 0:PASS], nc.sync)]
+        w2_s = [load_scales("w2_s0", w2_scales[:, :, 0:PASS])]
         w1_00 = load_w1(0, 0)
         w1_10 = load_w1(1, 0)
-        w1_20 = [
-            load_rows(w1[2 * PASS : K, c0 : c0 + HALF], tag="raw_half", bufs=2) for c0 in (0, HALF)
-        ]
-        gain_t = keep.tile([P, R_PASSES, PACK], F32, name="gain_t")
-        nc.sync.dma_start(out=gain_t[:], in_=gain.rearrange("(b p t) -> p b t", b=R_PASSES, t=PACK))
-        half_gain = keep.tile([P, R_PASSES, PACK], F32, name="half_gain")
-        nc.scalar.activation(out=half_gain[:], in_=gain_t[:], func=ACT.Copy, scale=0.5)
+        w1_20 = load_w1_halves(0)
         idx2 = load_list("idx2", offs2)
-        wgs_first = keep.tile([P, 1, S], F32, name="wgs_first")
-        wgs_rest = keep.tile([P, PACK - 1, S], F32, name="wgs_rest")
-        wgs_rows = wgs.rearrange("(m t) j -> m t j", t=PACK)
-        for q in (0, 2, 1, 3):
-            nc.sync.dma_start(out=wgs_first[32 * q : 32 * q + 32], in_=wgs_rows[:, 0:1, :])
-        wgs_t = [wgs_first[:, 0, :]] + [wgs_rest[:, t, :] for t in range(PACK - 1)]
-        pages = [[load_page0(0, 0)], []]
         w1_01 = load_w1(0, 1)
-        for q in (0, 2, 1, 3):
-            nc.sync.dma_start(out=wgs_rest[32 * q : 32 * q + 32], in_=wgs_rows[:, 1:PACK, :])
+        pages = [[load_page0(0, 0)], []]
         pages[0].append(load_page0(0, 1))
         w2_1 = load_w2(1)
-        w2_s.append(load_scales("w2_s1", w2_scales[:, :, PASS:H], nc.sync))
+        w2_s.append(load_scales("w2_s1", w2_scales[:, :, PASS:H]))
         w1_11 = load_w1(1, 1)
         pages[0].append(load_page0(0, 2))
-        w1_21 = load_w1(2, 1)
+        w1_21 = load_w1_halves(1)
         pages[0].append(load_page0(0, 3))
+
+        turned = bank_b.tile([P, J_TILES, P], F32, name="b", tag="b")
+        for jt in range(J_TILES):
+            nc.tensor.transpose(turned[:, jt, :], wgs_rows[:, jt * P : (jt + 1) * P], ident[:])
+        spread = ring.tile([P, J_TILES, PACK, 4, 32], F32, name="h", tag="h", bufs=2)
+        for q in range(4):
+            nc.scalar.copy(out=spread[:, :, :, q, :], in_=turned[:].rearrange("j s (m t) -> j s t m", t=PACK))
+        wgs_t = keep.tile([P, PACK, S], F32, name="wgs_t")
+        for t in range(PACK):
+            bank = bank_a.tile([P, S], F32, name="a", tag="a")
+            for jt in range(J_TILES):
+                nc.tensor.transpose(
+                    bank[:, jt * P : (jt + 1) * P], spread[:, jt, t].rearrange("j q m -> j (q m)"), ident[:]
+                )
+            nc.scalar.copy(out=wgs_t[:, t, :], in_=bank[:])
+        half_gain = keep.tile([P, R_PASSES, PACK], F32, name="half_gain")
+        nc.scalar.activation(out=half_gain[:], in_=gain_t[:], func=ACT.Copy, scale=0.5)
 
         v = [gather_table(a, words) for a, words in enumerate((tab0, tab1, tab2))]
         diff = open_difference(flat_stage(0, w2_0))
@@ -224,7 +238,7 @@ def tile_list_braille_proof_correction_kernel(
         idx4 = load_list("idx4", offs4)
         want0 = load_rows(want[0:PASS, :])
         pages[1].append(load_page0(1, 0))
-        w4_s = load_scales("w4_s", w4_scales, nc.sync)
+        w4_s = load_scales("w4_s", w4_scales)
         w4_t = keep.tile([P, R_PASSES, N], U32, name="w4_t", align_bytes=64)
         nc.sync.dma_start(out=w4_t[:].bitcast(I32), in_=w4_words.rearrange("a p c i -> p a (c i)").bitcast(I32))
         w3_0 = load_rows(w3[0:PASS, :])
@@ -242,20 +256,24 @@ def tile_list_braille_proof_correction_kernel(
             out_pages.append(tile)
 
         raised = [bank_b.tile([P, PASS], F32, name="b", tag="b") for jt in range(J_TILES)]
-        raised_pass(raised, 0, interleave(nc.scalar.copy, w1_01))
+        raised_pass(raised, 0, interleave(nc.vector.tensor_copy, w1_01))
         for t in range(PACK):
-            scatter(pages[0][t], idx2, h0[:, t, :], wgs_t[t])
+            scatter(pages[0][t], idx2, h0[:, t, :], wgs_t[:, t, :])
         diff = open_difference(flat_stage(1, w2_1))
         raised_pass(raised, 1, interleave(nc.scalar.copy, w1_11))
-        raised_pass(raised, 2, interleave(nc.scalar.copy, w1_21, tag="w1_last_then_x0", bufs=1))
+        for half in range(2):
+            tag, bufs = (("x1g", 2), ("w1_last_then_x0", 1))[half]
+            codes, scales = quantize(interleave(nc.scalar.copy, w1_21[half], tag=tag, bufs=bufs), "xq1", 2)
+            first_stage_pass(raised, 2, codes[:].bitcast(FP8X4), scales[:], half * HALF, HALF, half == 1)
         h1 = ring.tile([P, PACK, S], F32, name="h", tag="h", bufs=2)
-        close_difference(h1, 1, diff, half_tanh(raised, 0.5), 0, PACK)
+        close_difference(h1, 1, diff, half_tanh(raised, 0.5, 0, 1, "th_first", 4), 0, 1)
+        close_difference(h1, 1, diff, half_tanh(raised, 0.5, 1, PACK), 1, PACK)
         hq0 = quantize(interleave(nc.scalar.copy, h0), "hq", 2)
 
         x0 = ring.tile([P, PACK, S], F32, name="x0", tag="w1_last_then_x0", bufs=1, align_bytes=64)
         recall(x0, pages[0], want0, 0, S)
         for t in range(PACK):
-            scatter(pages[1][t], idx2, h1[:, t, :], wgs_t[t])
+            scatter(pages[1][t], idx2, h1[:, t, :], wgs_t[:, t, :])
         hq1 = quantize(interleave(nc.scalar.copy, h1, tag="h1_then_x0", bufs=1), "hq", 2)
         w3q = [quantize(interleave(nc.scalar.copy, raw), "w3q", 2) for raw in (w3_0, w3_1)]
         xq0 = quantize(interleave(nc.scalar.copy, x0, tag="h1_then_x0", bufs=1), "xq0", 1)
@@ -289,7 +307,8 @@ def tile_list_braille_proof_correction_kernel(
         for half in range(2):
             x1 = ring.tile([P, PACK, HALF], F32, name="h", tag="h", bufs=2)
             recall(x1, pages[1], want1, half * HALF, HALF)
-            xq1.append(quantize(interleave(nc.scalar.copy, x1, tag="x1g", bufs=2), "xq1", 2))
+            tag, bufs = (("x1g", 2), ("want1_then_factor", 1))[half]
+            xq1.append(quantize(interleave(nc.scalar.copy, x1, tag=tag, bufs=bufs), "xq1", 2))
         factor = ring.tile([P, N_TILES, S], F32, name="factor", tag="want1_then_factor", bufs=1, align_bytes=64)
         for n in range(N_TILES):
             nc.vector.tensor_tensor(factor[:, n, :], sway[n][:], wgo_t[:], ALU.mult)

from contextlib import ExitStack

import concourse.mybir as mybir
from concourse.masks import make_identity

K, T, S, H, T2, N = 1536, 2048, 512, 1024, 1024, 512
FLOPS = 2 * (2 * K * H * S + 2 * H * N * S)

F32 = mybir.dt.float32
BF16 = mybir.dt.bfloat16
I32 = mybir.dt.int32
U32 = mybir.dt.uint32
U16 = mybir.dt.uint16
U8 = mybir.dt.uint8
FP8X4 = mybir.dt.float8_e4m3fn_x4
FP4X4 = mybir.dt.float4_e2m1fn_x4
ALU = mybir.AluOpType
ACT = mybir.ActivationFunctionType

P = 128
PACK = 4
PASS = P * PACK
K_PASSES = K // PASS
R_PASSES = H // PASS
J_TILES = S // P
N_TILES = N // P
HALF = S // 2


def tile_list_braille_proof_correction_kernel(
    tc, tab_words, tab_scales, w1, w2_words, w2_scales, gain, wgs, page0, want, w3, w4_words, w4_scales,
    wgo, page1, offs, offs2, offs3, offs4, out,
):
    nc = tc.nc
    with ExitStack() as ctx:
        keep = ctx.enter_context(tc.tile_pool(name="keep", bufs=1))
        ring = ctx.enter_context(tc.tile_pool(name="ring", bufs=1))
        bank_a = ctx.enter_context(tc.psum_pool(name="bank_a", bufs=4))
        bank_b = ctx.enter_context(tc.psum_pool(name="bank_b", bufs=4))

        def load_list(name, src):
            tile = keep.tile([P, S // 16], U16, name=name)
            nc.sync.dma_start(tile[:], src)
            return tile

        def load_scales(name, src):
            passes, width = src.shape[0], src.shape[2]
            tile = keep.tile([P, passes * width], U8, name=name, align_bytes=64)
            nc.vector.memset(tile[:].bitcast(I32), 0)
            rows = src.rearrange("a (q r) c -> r q a c", r=4)
            for r in range(4):
                nc.sync.dma_start(
                    out=tile[r:P:32, :].bitcast(I32).rearrange("q (a c) -> q a c", a=passes),
                    in_=rows[r].bitcast(I32),
                )
            return tile

        def load_rows(src, tag="raw", bufs=3):
            tile = ring.tile([P, PACK, src.shape[1]], F32, name=tag, tag=tag, bufs=bufs, align_bytes=64)
            nc.sync.dma_start(out=tile[:], in_=src.rearrange("(p i) c -> p i c", i=PACK))
            return tile

        def interleave(engine_copy, raw, tag="grouped", bufs=3):
            width = raw.shape[2]
            grouped = ring.tile([P, width, PACK], BF16, name=tag, tag=tag, bufs=bufs, align_bytes=64)
            engine_copy(
                out=grouped[:].rearrange("p (c u) i -> p c i u", u=4),
                in_=raw[:].rearrange("p i (c u) -> p c i u", u=4),
            )
            return grouped

        def quantize(grouped, tag, bufs):
            width = grouped.shape[1]
            codes = ring.tile([P, width], U32, name=tag + "_codes", tag=tag + "_codes", bufs=bufs, align_bytes=64)
            scales = ring.tile([P, width], U8, name=tag + "_scales", tag=tag + "_scales", bufs=bufs, align_bytes=64)
            nc.vector.quantize_mx(
                out=codes[:].bitcast(FP8X4), scales=scales[:], in_=grouped[:].rearrange("p c i -> p (c i)")
            )
            return codes, scales

        def load_table(a):
            tile = keep.tile([P, T], U32, name="tab%d" % a, align_bytes=64)
            nc.sync.dma_start(out=tile[:].bitcast(I32), in_=tab_words[a].rearrange("p t i -> p (t i)").bitcast(I32))
            return tile

        def gather_table(a, words):
            v_codes = keep.tile([P, S], U32, name="v_codes%d" % a, align_bytes=64)
            nc.vector.tensor_copy(v_codes[:], words[:].indirect(idx[:]))
            v_scale = keep.tile([P, S], U8, name="v_scale%d" % a, align_bytes=64)
            nc.vector.tensor_copy(v_scale[:], tab_s[:, a * T : (a + 1) * T].indirect(idx[:]))
            return v_codes, v_scale

        def load_w1(a, b):
            return load_rows(w1[a * PASS : (a + 1) * PASS, b * PASS : (b + 1) * PASS])

        def load_w1_halves(b):
            return [
                load_rows(w1[2 * PASS : K, c0 : c0 + HALF], tag="raw_half", bufs=2)
                for c0 in (b * PASS, b * PASS + HALF)
            ]

        def load_w2(b):
            tile = keep.tile([P, K_PASSES, 2 * PASS], U8, name="w2_%d" % b, align_bytes=64)
            nc.sync.dma_start(
                out=tile[:].bitcast(I32),
                in_=w2_words[:, :, 2 * PASS * b : 2 * PASS * (b + 1)].rearrange("a p c -> p a c").bitcast(I32),
            )
            return tile

        def load_page0(b, t):
            tile = keep.tile([P, T2], F32, name="page0_%d_%d" % (b, t))
            nc.sync.dma_start(
                out=tile[:], in_=page0[b * PASS : (b + 1) * PASS, :].rearrange("(p t) c -> t p c", t=PACK)[t]
            )
            return tile

        def first_stage_pass(banks, a, w_codes, w_scale, r0=0, width=PASS, stop=None):
            v_codes, v_scale = v[a]
            for jt in range(J_TILES):
                cols = slice(jt * P, (jt + 1) * P)
                nc.tensor.matmul_mx(
                    out=banks[jt][:, r0 : r0 + width], lhsT=v_codes[:, cols].bitcast(FP8X4),
                    lhsT_scale=v_scale[:, cols], rhs=w_codes, rhs_scale=w_scale, start=(a == 0),
                    stop=(a == K_PASSES - 1 if stop is None else stop),
                )

        def half_tanh(banks, scale, t0=0, t1=PACK, tag="th", bufs=8):
            tiles = []
            for bank in banks:
                tile = ring.tile([P, t1 - t0, P], F32, name=tag, tag=tag, bufs=bufs)
                nc.scalar.activation(
                    out=tile[:], in_=bank[:].rearrange("j (m t) -> j t m", t=PACK)[:, t0:t1, :], func=ACT.Tanh,
                    scale=scale,
                )
                tiles.append(tile)
            return tiles

        def flat_stage(b, w2_tile):
            banks = [bank_a.tile([P, PASS], F32, name="a", tag="a") for jt in range(J_TILES)]
            for a in range(K_PASSES):
                first_stage_pass(
                    banks, a, w2_tile[:, a, :].bitcast(FP4X4), w2_s[b][:, a * PASS : (a + 1) * PASS]
                )
            return half_tanh(banks, -0.5)

        def raised_pass(banks, a, grouped):
            codes, scales = quantize(grouped, "w1q", 3)
            first_stage_pass(banks, a, codes[:].bitcast(FP8X4), scales[:])

        def open_difference(th_flat):
            banks = [bank_a.tile([P, S], F32, name="a", tag="a") for t in range(PACK)]
            for t in range(PACK):
                for jt in range(J_TILES):
                    nc.tensor.matmul(
                        banks[t][:, jt * P : (jt + 1) * P], th_flat[jt][:, t, :], ident[:],
                        start=(jt == 0), stop=False, is_transpose=True,
                    )
            return banks

        def close_difference(h, b, banks, th_raised, t0, t1):
            for t in range(t0, t1):
                for jt in range(J_TILES):
                    nc.tensor.matmul(
                        banks[t][:, jt * P : (jt + 1) * P], th_raised[jt][:, t - t0, :], ident[:],
                        start=False, stop=(jt == J_TILES - 1), is_transpose=True,
                    )
                nc.scalar.activation(
                    out=h[:, t, :], in_=banks[t][:], func=ACT.Copy, scale=half_gain[:, b, t : t + 1]
                )

        def scatter(page, offsets, values, weights):
            nc.vector.tensor_tensor(page[:].indirect(offsets[:]), values, weights, ALU.mult)

        def recall(x, pages, wanted, j0, width):
            for t in range(PACK):
                nc.vector.tensor_tensor(
                    x[:, t, :], pages[t][:].indirect(idx3[:, j0 // 16 : (j0 + width) // 16]),
                    wanted[:, t, j0 : j0 + width], ALU.subtract,
                )

        idx = load_list("idx", offs)
        tab0 = load_table(0)
        tab_s = load_scales("tab_s", tab_scales)
        wgs_rows = ring.tile([P, S], F32, name="th", tag="th", bufs=8)
        nc.sync.dma_start(out=wgs_rows[:], in_=wgs)
        ident = keep.tile([P, P], F32, name="ident")
        make_identity(nc, ident[:])
        gain_t = keep.tile([P, R_PASSES, PACK], F32, name="gain_t")
        nc.gpsimd.dma_start(out=gain_t[:], in_=gain.rearrange("(b p t) -> p b t", b=R_PASSES, t=PACK))
        tab1 = load_table(1)
        tab2 = load_table(2)
        w2_0 = load_w2(0)
        w2_s = [load_scales("w2_s0", w2_scales[:, :, 0:PASS])]
        w1_00 = load_w1(0, 0)
        w1_10 = load_w1(1, 0)
        w1_20 = load_w1_halves(0)
        idx2 = load_list("idx2", offs2)
        w1_01 = load_w1(0, 1)
        pages = [[load_page0(0, 0)], []]
        pages[0].append(load_page0(0, 1))
        w2_1 = load_w2(1)
        w2_s.append(load_scales("w2_s1", w2_scales[:, :, PASS:H]))
        w1_11 = load_w1(1, 1)
        pages[0].append(load_page0(0, 2))
        w1_21 = load_w1_halves(1)
        pages[0].append(load_page0(0, 3))

        turned = bank_b.tile([P, J_TILES, P], F32, name="b", tag="b")
        for jt in range(J_TILES):
            nc.tensor.transpose(turned[:, jt, :], wgs_rows[:, jt * P : (jt + 1) * P], ident[:])
        spread = ring.tile([P, J_TILES, PACK, 4, 32], F32, name="h", tag="h", bufs=2)
        for q in range(4):
            nc.scalar.copy(out=spread[:, :, :, q, :], in_=turned[:].rearrange("j s (m t) -> j s t m", t=PACK))
        wgs_t = keep.tile([P, PACK, S], F32, name="wgs_t")
        for t in range(PACK):
            bank = bank_a.tile([P, S], F32, name="a", tag="a")
            for jt in range(J_TILES):
                nc.tensor.transpose(
                    bank[:, jt * P : (jt + 1) * P], spread[:, jt, t].rearrange("j q m -> j (q m)"), ident[:]
                )
            nc.scalar.copy(out=wgs_t[:, t, :], in_=bank[:])
        half_gain = keep.tile([P, R_PASSES, PACK], F32, name="half_gain")
        nc.scalar.activation(out=half_gain[:], in_=gain_t[:], func=ACT.Copy, scale=0.5)

        v = [gather_table(a, words) for a, words in enumerate((tab0, tab1, tab2))]
        diff = open_difference(flat_stage(0, w2_0))
        raised = [bank_b.tile([P, PASS], F32, name="b", tag="b") for jt in range(J_TILES)]
        raised_pass(raised, 0, interleave(nc.vector.tensor_copy, w1_00))
        raised_pass(raised, 1, interleave(nc.vector.tensor_copy, w1_10))
        for half in range(2):
            codes, scales = quantize(interleave(nc.vector.tensor_copy, w1_20[half], tag="x1g", bufs=2), "xq1", 2)
            first_stage_pass(raised, 2, codes[:].bitcast(FP8X4), scales[:], half * HALF, HALF, half == 1)
        h0 = ring.tile([P, PACK, S], F32, name="h", tag="h", bufs=2)
        close_difference(h0, 0, diff, half_tanh(raised, 0.5, 0, 1, "th_first", 4), 0, 1)
        close_difference(h0, 0, diff, half_tanh(raised, 0.5, 1, PACK), 1, PACK)

        idx3 = load_list("idx3", offs3)
        idx4 = load_list("idx4", offs4)
        want0 = load_rows(want[0:PASS, :])
        pages[1].append(load_page0(1, 0))
        w4_s = load_scales("w4_s", w4_scales)
        w4_t = keep.tile([P, R_PASSES, N], U32, name="w4_t", align_bytes=64)
        nc.sync.dma_start(out=w4_t[:].bitcast(I32), in_=w4_words.rearrange("a p c i -> p a (c i)").bitcast(I32))
        w3_0 = load_rows(w3[0:PASS, :])
        pages[1].append(load_page0(1, 1))
        pages[1].append(load_page0(1, 2))
        w3_1 = load_rows(w3[PASS:H, :])
        pages[1].append(load_page0(1, 3))
        want1 = load_rows(want[PASS:H, :], tag="want1_then_factor", bufs=1)
        wgo_t = keep.tile([P, S], F32, name="wgo_t")
        nc.sync.dma_start(out=wgo_t[:], in_=wgo)
        out_pages = []
        for n in range(N_TILES):
            tile = keep.tile([P, T2], F32, name="page1_%d" % n)
            nc.sync.dma_start(out=tile[:], in_=page1[n * P : (n + 1) * P, :])
            out_pages.append(tile)

        raised = [bank_b.tile([P, PASS], F32, name="b", tag="b") for jt in range(J_TILES)]
        raised_pass(raised, 0, interleave(nc.vector.tensor_copy, w1_01))
        for t in range(PACK):
            scatter(pages[0][t], idx2, h0[:, t, :], wgs_t[:, t, :])
        diff = open_difference(flat_stage(1, w2_1))
        raised_pass(raised, 1, interleave(nc.scalar.copy, w1_11))
        for half in range(2):
            tag, bufs = (("x1g", 2), ("w1_last_then_x0", 1))[half]
            codes, scales = quantize(interleave(nc.scalar.copy, w1_21[half], tag=tag, bufs=bufs), "xq1", 2)
            first_stage_pass(raised, 2, codes[:].bitcast(FP8X4), scales[:], half * HALF, HALF, half == 1)
        h1 = ring.tile([P, PACK, S], F32, name="h", tag="h", bufs=2)
        close_difference(h1, 1, diff, half_tanh(raised, 0.5, 0, 1, "th_first", 4), 0, 1)
        close_difference(h1, 1, diff, half_tanh(raised, 0.5, 1, PACK), 1, PACK)
        hq0 = quantize(interleave(nc.scalar.copy, h0), "hq", 2)

        x0 = ring.tile([P, PACK, S], F32, name="x0", tag="w1_last_then_x0", bufs=1, align_bytes=64)
        recall(x0, pages[0], want0, 0, S)
        for t in range(PACK):
            scatter(pages[1][t], idx2, h1[:, t, :], wgs_t[:, t, :])
        hq1 = quantize(interleave(nc.scalar.copy, h1, tag="h1_then_x0", bufs=1), "hq", 2)
        w3q = [quantize(interleave(nc.scalar.copy, raw), "w3q", 2) for raw in (w3_0, w3_1)]
        xq0 = quantize(interleave(nc.scalar.copy, x0, tag="h1_then_x0", bufs=1), "xq0", 1)

        sway = []
        for n in range(N_TILES):
            cols = slice(n * P, (n + 1) * P)
            bank = bank_b.tile([P, S], F32, name="b", tag="b")
            for b, (codes, scales) in enumerate((hq0, hq1)):
                nc.tensor.matmul_mx(
                    out=bank[:], lhsT=w4_t[:, b, cols].bitcast(FP8X4),
                    lhsT_scale=w4_s[:, b * N + n * P : b * N + (n + 1) * P],
                    rhs=codes[:].bitcast(FP8X4), rhs_scale=scales[:], start=(b == 0), stop=(b == R_PASSES - 1),
                )
            tile = ring.tile([P, S], F32, name="th", tag="th", bufs=8)
            nc.scalar.activation(out=tile[:], in_=bank[:], func=ACT.Tanh)
            sway.append(tile)

        def fix_pass(bank, n, b, xq, j0, width, start, stop):
            cols = slice(n * P, (n + 1) * P)
            nc.tensor.matmul_mx(
                out=bank[:, j0 : j0 + width], lhsT=w3q[b][0][:, cols].bitcast(FP8X4), lhsT_scale=w3q[b][1][:, cols],
                rhs=xq[0][:].bitcast(FP8X4), rhs_scale=xq[1][:], start=start, stop=stop,
            )

        fix = [bank_a.tile([P, S], F32, name="a", tag="a") for n in range(N_TILES)]
        for n in range(N_TILES):
            fix_pass(fix[n], n, 0, xq0, 0, S, True, False)

        xq1 = []
        for half in range(2):
            x1 = ring.tile([P, PACK, HALF], F32, name="h", tag="h", bufs=2)
            recall(x1, pages[1], want1, half * HALF, HALF)
            tag, bufs = (("x1g", 2), ("want1_then_factor", 1))[half]
            xq1.append(quantize(interleave(nc.scalar.copy, x1, tag=tag, bufs=bufs), "xq1", 2))
        factor = ring.tile([P, N_TILES, S], F32, name="factor", tag="want1_then_factor", bufs=1, align_bytes=64)
        for n in range(N_TILES):
            nc.vector.tensor_tensor(factor[:, n, :], sway[n][:], wgo_t[:], ALU.mult)
        for half in range(2):
            for n in range(N_TILES):
                fix_pass(fix[n], n, 1, xq1[half], half * HALF, HALF, False, half == 1)
        for n in range(N_TILES):
            fix_sb = ring.tile([P, S], F32, name="th", tag="th", bufs=8)
            nc.scalar.copy(out=fix_sb[:], in_=fix[n][:])
            scatter(out_pages[n], idx4, fix_sb[:], factor[:, n, :])
            nc.sync.dma_start(out=out[n * P : (n + 1) * P, :], in_=out_pages[n][:])
